import numpy as np
import ml_dtypes


def mxq(x, axis, fmt="e4m3"):
    dtype, down = {"e4m3": (ml_dtypes.float8_e4m3fn, 7), "e5m2": (ml_dtypes.float8_e5m2, 14)}[fmt]
    v = np.moveaxis(np.asarray(x, np.float32).astype(ml_dtypes.bfloat16).astype(np.float64), axis, -1)
    blocks = v.reshape(v.shape[:-1] + (-1, 32))
    amax = np.abs(blocks).max(-1, keepdims=True)
    byte = np.maximum(np.where(amax > 0, np.frexp(amax)[1] - 1 + 127, 0) - down, 1)
    scale = np.exp2(byte - 127.0)
    codes = (blocks / scale).astype(np.float32).astype(dtype).astype(np.float64)
    return np.moveaxis((codes * scale).reshape(v.shape), -1, axis)


WIDE = False


def mx_kscale(k):
    if not WIDE:
        return np.ones(k)
    levels = np.array([10, -10, 5, -5, 0])
    if k % 512:
        return np.exp2(np.random.permutation(np.resize(levels, k // 32))).repeat(32)
    a = np.empty((k // 512, 16))
    for p in range(k // 512):
        a[p, :8] = np.random.permutation(np.resize(levels, 8))
        for g in range(8):
            far = levels[np.abs(levels - a[p, g]) >= 10]
            a[p, g + 8] = far[np.random.randint(len(far))]
    return np.exp2(a.ravel()).repeat(32)


def f64(x):
    return np.asarray(x).astype(np.float64)


def striped8(idx):
    return np.asarray(idx).reshape(8, -1, 16).transpose(0, 2, 1).reshape(128, -1).astype(np.uint16)


def unstriped8(offs):
    return offs.reshape(8, 16, -1).transpose(0, 2, 1).reshape(8, -1).astype(np.int64)


def pick8(x, idx, run):
    r = np.arange(len(x))
    return x[r[:, None], idx[r % (8 * run) // run]]


E2M1 = np.array([0.0, 0.5, 1.0, 1.5, 2.0, 3.0, 4.0, 6.0, -0.0, -0.5, -1.0, -1.5, -2.0, -3.0, -4.0, -6.0])


def pack_weight(w, fmt):
    k, n = w.shape
    w = f64(np.asarray(w, np.float32).astype(ml_dtypes.bfloat16)).reshape(k // 32, 32, n)
    amax = np.abs(w).max(1)
    if fmt == "e4m3":
        byte = np.frexp(amax)[1] - 1 + 127 - 7
    else:
        mant, ex = np.frexp(amax / 6.0)
        byte = np.where(mant > 0.5, ex, ex - 1) + 127
    byte = np.clip(np.where(amax > 0, byte, 1), 1, 254)
    scaled = (w * np.exp2(127.0 - byte)[:, None, :]).reshape(k, n).astype(np.float32)
    by_word = np.ascontiguousarray(scaled.reshape(k // 512, 128, 4, n).transpose(0, 1, 3, 2))
    if fmt == "e4m3":
        words = by_word.astype(ml_dtypes.float8_e4m3fn).view(np.uint8)
    else:
        c = by_word.astype(ml_dtypes.float4_e2m1fn).view(np.uint8) & 0xF
        words = (c[..., 0::2] | (c[..., 1::2] << 4)).reshape(k // 512, 128, 2 * n)
    return np.ascontiguousarray(words), np.ascontiguousarray(byte.astype(np.uint8).reshape(k // 512, 16, n))


def unpack_weight(words, scales, fmt):
    g, _, n = scales.shape
    words = np.ascontiguousarray(words).reshape(g, 128, n, -1)
    if fmt == "e4m3":
        vals = words.view(ml_dtypes.float8_e4m3fn).astype(np.float64)
    else:
        nib = np.empty((g, 128, n, 4), np.uint8)
        nib[..., 0::2] = words & 0xF
        nib[..., 1::2] = words >> 4
        vals = E2M1[nib]
    vals = vals * np.repeat(np.exp2(scales.astype(np.float64) - 127.0), 8, axis=1)[..., None]
    return vals.transpose(0, 1, 3, 2).reshape(g * 512, n)


D, K, T, U, X, S, I, Q = 512, 512, 1024, 1024, 1024, 1024, 512, 128


def setup_inputs():
    n = np.random.standard_normal
    idx = np.stack([np.random.permutation(T)[:I] for _ in range(8)])
    idx2 = np.stack([np.random.permutation(U)[:I] for _ in range(8)])
    idx3 = np.stack([np.random.permutation(X)[:I] for _ in range(8)])
    idx4 = np.stack([np.random.permutation(X)[:I] for _ in range(8)])
    idx5 = np.stack([np.random.permutation(X)[:I] for _ in range(8)])
    idx6 = np.stack([np.random.permutation(S)[:I] for _ in range(8)])
    idx7 = np.stack([np.random.permutation(S)[:I] for _ in range(8)])
    fd = mx_kscale(D)
    fk = mx_kscale(K)
    wqp = pack_weight(n((D, K)) * 1.0 / np.sqrt(D) * fd[:, None] * fk, "e4m3")
    keysp = pack_weight(n((K, T)) * 1.0 / np.sqrt(K) / fk[:, None], "e2m1")
    notesp = pack_weight(n((K, U)) * 1.0 / np.sqrt(K) / fk[:, None], "e4m3")
    usersp = pack_weight(n((D, X)) * 1.0 / np.sqrt(D) * fd[:, None], "e2m1")
    shelvesp = pack_weight(n((D, S)) * 1.0 / np.sqrt(D) * fd[:, None], "e4m3")
    return {
        "states": (n((D, Q)) * 0.95 / fd[:, None]).astype(np.float32),
        "wq_words": wqp[0],
        "wq_scales": wqp[1],
        "keys_words": keysp[0],
        "keys_scales": keysp[1],
        "notes_words": notesp[0],
        "notes_scales": notesp[1],
        "users_words": usersp[0],
        "users_scales": usersp[1],
        "shelves_words": shelvesp[0],
        "shelves_scales": shelvesp[1],
        "offs": striped8(idx),
        "offs2": striped8(idx2),
        "offs3": striped8(idx3),
        "offs4": striped8(idx4),
        "offs5": striped8(idx5),
        "offs6": striped8(idx6),
        "offs7": striped8(idx7),
    }


def reference(states, wq_words, wq_scales, keys_words, keys_scales, notes_words, notes_scales, users_words, users_scales, shelves_words, shelves_scales, offs, offs2, offs3, offs4, offs5, offs6, offs7):
    idx = unstriped8(offs)
    idx2 = unstriped8(offs2)
    idx3 = unstriped8(offs3)
    idx4 = unstriped8(offs4)
    idx5 = unstriped8(offs5)
    idx6 = unstriped8(offs6)
    idx7 = unstriped8(offs7)
    wqu = unpack_weight(wq_words, wq_scales, "e4m3")
    keysu = unpack_weight(keys_words, keys_scales, "e2m1")
    notesu = unpack_weight(notes_words, notes_scales, "e4m3")
    usersu = unpack_weight(users_words, users_scales, "e2m1")
    shelvesu = unpack_weight(shelves_words, shelves_scales, "e4m3")
    statesq = mxq(f64(states), 0, "e4m3")
    qv = wqu.T @ statesq
    qvq = mxq(qv, 0, "e4m3")
    a = qvq.T @ keysu
    b = qvq.T @ notesu
    c0 = statesq.T @ usersu
    d0 = statesq.T @ shelvesu
    f1 = np.zeros((Q, X))
    f1[np.arange(Q)[:, None], idx3[np.arange(Q) % 128 // 16]] = pick8(a, idx, 16)
    f2 = np.zeros((Q, X))
    f2[np.arange(Q)[:, None], idx4[np.arange(Q) % 128 // 16]] = pick8(b, idx2, 16)
    m1 = np.minimum(f1, f2)
    cc = c0 + m1
    f3 = np.zeros((Q, S))
    f3[np.arange(Q)[:, None], idx6[np.arange(Q) % 128 // 16]] = pick8(cc, idx5, 16)
    dd = d0 - f3
    y = pick8(dd, idx7, 16)
    return y

@@ -1,0 +1,181 @@
+from contextlib import ExitStack
+
+import concourse.mybir as mybir
+
+D, K, T, I, Q = 512, 512, 1024, 512, 128
+FLOPS = 2 * D * K * Q + 4 * 2 * K * Q * T
+
+F32 = mybir.dt.float32
+BF16 = mybir.dt.bfloat16
+I32 = mybir.dt.int32
+U32 = mybir.dt.uint32
+U16 = mybir.dt.uint16
+U8 = mybir.dt.uint8
+FP8X4 = mybir.dt.float8_e4m3fn_x4
+FP4X4 = mybir.dt.float4_e2m1fn_x4
+COPY = mybir.ActivationFunctionType.Copy
+ALU = mybir.AluOpType
+
+P = 128
+PACK = 4
+BANK = 512
+HALF = I // 2
+
+
+def tile_attend_tributaries_madefour_kernel(
+    tc, states, wq_words, wq_scales, keys_words, keys_scales, notes_words, notes_scales,
+    users_words, users_scales, shelves_words, shelves_scales,
+    offs, offs2, offs3, offs4, offs5, offs6, offs7, out,
+):
+    nc = tc.nc
+    with ExitStack() as ctx:
+        sb = ctx.enter_context(tc.tile_pool(name="sb", bufs=1))
+        ps = ctx.enter_context(tc.psum_pool(name="ps", bufs=1))
+
+        def zeroed_plane(name, width):
+            plane = sb.tile([P, width], U8, name=name, align_bytes=64)
+            nc.vector.memset(plane[:].bitcast(I32), 0)
+            return plane
+
+        def load_scales(queue, plane, scales):
+            for quad in range(4):
+                queue.dma_start(
+                    plane[32 * quad : 32 * quad + 4, :].bitcast(I32),
+                    scales[0, 4 * quad : 4 * quad + 4, :].bitcast(I32),
+                )
+
+        def load_fp8(name, words, width):
+            codes = sb.tile([P, width], U32, name=name, align_bytes=64)
+            nc.sync.dma_start(codes[:].bitcast(I32), words[0].rearrange("p n t -> p (n t)").bitcast(I32))
+            return codes
+
+        def load_fp4(name, words):
+            codes = sb.tile([P, 2 * T], U8, name=name, align_bytes=64)
+            nc.sync.dma_start(codes[:].bitcast(I32), words[0].bitcast(I32))
+            return codes
+
+        def load_list(name, src):
+            lst = sb.tile([P, I // 16], U16, name=name)
+            nc.sync.dma_start(lst[:], src)
+            return lst
+
+        wq_raw_s = zeroed_plane("wq_raw_s", K)
+        keys_s = zeroed_plane("keys_s", T)
+        notes_s = zeroed_plane("notes_s", T)
+        users_s = zeroed_plane("users_s", T)
+        shelves_s = zeroed_plane("shelves_s", T)
+        f1 = sb.tile([P, T], F32, name="f1")
+        f2 = sb.tile([P, T], F32, name="f2")
+        f3 = sb.tile([P, T], F32, name="f3")
+        nc.vector.memset(f1[:], 0.0)
+        nc.gpsimd.memset(f2[:], 0.0)
+        nc.gpsimd.memset(f3[:], 0.0)
+
+        st_raw = sb.tile([P, PACK, Q], F32, name="st_raw")
+        nc.sync.dma_start(st_raw[:], states.rearrange("(p j) q -> p j q", j=PACK))
+        wq_raw = load_fp8("wq_raw", wq_words, K)
+        load_scales(nc.scalar, wq_raw_s, wq_scales)
+        keys = load_fp4("keys", keys_words)
+        load_scales(nc.sync, keys_s, keys_scales)
+        l1 = load_list("l1", offs)
+        l3 = load_list("l3", offs3)
+        notes = load_fp8("notes", notes_words, T)
+        load_scales(nc.sync, notes_s, notes_scales)
+        l2 = load_list("l2", offs2)
+        l4 = load_list("l4", offs4)
+        users = load_fp4("users", users_words)
+        load_scales(nc.sync, users_s, users_scales)
+        l5 = load_list("l5", offs5)
+        l6 = load_list("l6", offs6)
+        shelves = load_fp8("shelves", shelves_words, T)
+        load_scales(nc.sync, shelves_s, shelves_scales)
+        l7 = load_list("l7", offs7)
+
+        st_bf = sb.tile([P, Q, PACK], BF16, name="st_bf", align_bytes=64)
+        nc.vector.tensor_copy(
+            st_bf[:].rearrange("p (c i) t -> p c t i", i=4),
+            st_raw[:].rearrange("p t (c i) -> p c t i", i=4),
+        )
+        wq = sb.tile([P, K], U32, name="wq", align_bytes=64)
+        nc.scalar.copy(
+            wq[:].rearrange("p (t c i) -> p c t i", t=PACK, i=4),
+            wq_raw[:].rearrange("p (c i t) -> p c t i", t=PACK, i=4),
+        )
+        wq_s = sb.tile([P, K], U8, name="wq_s", align_bytes=64)
+        nc.vector.tensor_copy(
+            wq_s[:].rearrange("p (t c i) -> p c t i", t=PACK, i=16),
+            wq_raw_s[:].rearrange("p (c i t) -> p c t i", t=PACK, i=16),
+        )
+        st = sb.tile([P, Q], U32, name="st", align_bytes=64)
+        st_s = sb.tile([P, Q], U8, name="st_s", align_bytes=64)
+        nc.vector.quantize_mx(st[:].bitcast(FP8X4), st_s[:], st_bf[:].rearrange("p q t -> p (q t)"))
+
+        qv_ps = ps.tile([P, PACK, Q], F32, name="qv_ps")
+        for t in range(PACK):
+            cols = slice(t * P, (t + 1) * P)
+            nc.tensor.matmul_mx(
+                qv_ps[:, t, :], lhsT=wq[:, cols].bitcast(FP8X4), lhsT_scale=wq_s[:, cols],
+                rhs=st[:].bitcast(FP8X4), rhs_scale=st_s[:], start=True, stop=True,
+            )
+        qv_bf = sb.tile([P, Q, PACK], BF16, name="qv_bf", align_bytes=64)
+        nc.vector.tensor_copy(qv_bf[:], qv_ps[:].rearrange("p t q -> p q t"))
+        qv = sb.tile([P, Q], U32, name="qv", align_bytes=64)
+        qv_s = sb.tile([P, Q], U8, name="qv_s", align_bytes=64)
+        nc.vector.quantize_mx(qv[:].bitcast(FP8X4), qv_s[:], qv_bf[:].rearrange("p q t -> p (q t)"))
+
+        def scores(tag, rows, rows_s, table, table_s, fp4, c0, c1):
+            bank = ps.tile([P, c1 - c0], F32, name=tag + str(c0), tag=tag)
+            moving = table[:, 2 * c0 : 2 * c1].bitcast(FP4X4) if fp4 else table[:, c0:c1].bitcast(FP8X4)
+            nc.tensor.matmul_mx(
+                bank[:], lhsT=rows[:].bitcast(FP8X4), lhsT_scale=rows_s[:],
+                rhs=moving, rhs_scale=table_s[:, c0:c1], start=True, stop=True,
+            )
+            return bank
+
+        def gather_halves(dst, window, lst):
+            cols = HALF // 16
+            nc.vector.tensor_copy(dst[:, :HALF], window[:].indirect(lst[:, :cols]))
+            nc.scalar.activation(dst[:, HALF:], window[:].indirect(lst[:, cols:]), COPY)
+
+        a = sb.tile([P, T], F32, name="a")
+        a0 = scores("bank_x", qv, qv_s, keys, keys_s, True, 0, 512)
+        a1 = scores("bank_y", qv, qv_s, keys, keys_s, True, 512, 768)
+        a2 = scores("bank_z", qv, qv_s, keys, keys_s, True, 768, 1024)
+        nc.vector.tensor_copy(a[:, 0:512], a0[:])
+        nc.scalar.activation(a[:, 512:768], a1[:], COPY)
+        nc.scalar.activation(a[:, 768:1024], a2[:], COPY)
+        ga = sb.tile([P, I], F32, name="ga")
+        gather_halves(ga, a, l1)
+        nc.vector.tensor_copy(f1[:].indirect(l3[:]), ga[:])
+
+        b = sb.tile([P, T], F32, name="b")
+        for h in range(2):
+            bank = scores("bank_b%d" % h, qv, qv_s, notes, notes_s, False, h * BANK, (h + 1) * BANK)
+            nc.scalar.activation(b[:, h * BANK : (h + 1) * BANK], bank[:], COPY)
+        gb = sb.tile([P, I], F32, name="gb")
+        nc.scalar.activation(gb[:], b[:].indirect(l2[:]), COPY)
+        nc.vector.tensor_copy(f2[:].indirect(l4[:]), gb[:])
+
+        c_banks = [scores("bank_c%d" % h, st, st_s, users, users_s, True, h * BANK, (h + 1) * BANK) for h in range(2)]
+        m1 = sb.tile([P, T], F32, name="m1")
+        cc = sb.tile([P, T], F32, name="cc")
+        halves = [slice(h * BANK, (h + 1) * BANK) for h in range(2)]
+        for h in range(2):
+            nc.vector.tensor_tensor(m1[:, halves[h]], f1[:, halves[h]], f2[:, halves[h]], ALU.min)
+        for h in range(2):
+            nc.vector.tensor_tensor(cc[:, halves[h]], c_banks[h][:], m1[:, halves[h]], ALU.add)
+        gc = sb.tile([P, I], F32, name="gc")
+        gather_halves(gc, cc, l5)
+        nc.vector.tensor_copy(f3[:].indirect(l6[:]), gc[:])
+
+        d_banks = [
+            scores(tag, st, st_s, shelves, shelves_s, False, h * BANK, (h + 1) * BANK)
+            for h, tag in enumerate(("bank_x", "bank_y"))
+        ]
+        dd = sb.tile([P, T], F32, name="dd")
+        for h in range(2):
+            nc.vector.tensor_tensor(dd[:, halves[h]], d_banks[h][:], f3[:, halves[h]], ALU.subtract)
+        y = sb.tile([P, I], F32, name="y")
+        gather_halves(y, dd, l7)
+        nc.sync.dma_start(out[:, :HALF], y[:, :HALF])
+        nc.scalar.dma_start(out[:, HALF:], y[:, HALF:])

@@ -30,11 +30,12 @@ def tile_attend_tributaries_madefour_kernel(
     nc = tc.nc
     with ExitStack() as ctx:
         sb = ctx.enter_context(tc.tile_pool(name="sb", bufs=1))
+        shared = ctx.enter_context(tc.tile_pool(name="shared", bufs=1))
         ps = ctx.enter_context(tc.psum_pool(name="ps", bufs=1))
 
-        def zeroed_plane(name, width):
+        def zeroed_plane(engine, name, width):
             plane = sb.tile([P, width], U8, name=name, align_bytes=64)
-            nc.vector.memset(plane[:].bitcast(I32), 0)
+            engine.memset(plane[:].bitcast(I32), 0)
             return plane
 
         def load_scales(queue, plane, scales):
@@ -59,24 +60,21 @@ def tile_attend_tributaries_madefour_kernel(
             nc.sync.dma_start(lst[:], src)
             return lst
 
-        wq_raw_s = zeroed_plane("wq_raw_s", K)
-        keys_s = zeroed_plane("keys_s", T)
-        notes_s = zeroed_plane("notes_s", T)
-        users_s = zeroed_plane("users_s", T)
-        shelves_s = zeroed_plane("shelves_s", T)
+        wq_raw_s = shared.tile([P, K], U8, name="wq_raw_s", align_bytes=64, offset=0)
+        nc.gpsimd.memset(wq_raw_s[:].bitcast(I32), 0)
+        keys_s = zeroed_plane(nc.gpsimd, "keys_s", T)
+        notes_s = zeroed_plane(nc.vector, "notes_s", T)
+        users_s = zeroed_plane(nc.vector, "users_s", T)
+        shelves_s = zeroed_plane(nc.vector, "shelves_s", T)
         f1 = sb.tile([P, T], F32, name="f1")
-        f2 = sb.tile([P, T], F32, name="f2")
-        f3 = sb.tile([P, T], F32, name="f3")
         nc.vector.memset(f1[:], 0.0)
-        nc.gpsimd.memset(f2[:], 0.0)
-        nc.gpsimd.memset(f3[:], 0.0)
 
         st_raw = sb.tile([P, PACK, Q], F32, name="st_raw")
         nc.sync.dma_start(st_raw[:], states.rearrange("(p j) q -> p j q", j=PACK))
+        load_scales(nc.sync, wq_raw_s, wq_scales)
         wq_raw = load_fp8("wq_raw", wq_words, K)
-        load_scales(nc.scalar, wq_raw_s, wq_scales)
-        keys = load_fp4("keys", keys_words)
         load_scales(nc.sync, keys_s, keys_scales)
+        keys = load_fp4("keys", keys_words)
         l1 = load_list("l1", offs)
         l3 = load_list("l3", offs3)
         notes = load_fp8("notes", notes_words, T)
@@ -91,16 +89,17 @@ def tile_attend_tributaries_madefour_kernel(
         load_scales(nc.sync, shelves_s, shelves_scales)
         l7 = load_list("l7", offs7)
 
-        st_bf = sb.tile([P, Q, PACK], BF16, name="st_bf", align_bytes=64)
+        st_bf = shared.tile([P, Q, PACK], BF16, name="st_bf", align_bytes=64, offset=K)
         nc.vector.tensor_copy(
             st_bf[:].rearrange("p (c i) t -> p c t i", i=4),
             st_raw[:].rearrange("p t (c i) -> p c t i", i=4),
         )
         wq = sb.tile([P, K], U32, name="wq", align_bytes=64)
-        nc.scalar.copy(
-            wq[:].rearrange("p (t c i) -> p c t i", t=PACK, i=4),
-            wq_raw[:].rearrange("p (c i t) -> p c t i", t=PACK, i=4),
-        )
+        for pair in range(2):
+            nc.scalar.copy(
+                wq[:, 256 * pair : 256 * (pair + 1)].rearrange("p (t c i) -> p c t i", t=2, i=4),
+                wq_raw[:].rearrange("p (c i t) -> p c t i", t=PACK, i=4)[:, :, 2 * pair : 2 * pair + 2, :],
+            )
         wq_s = sb.tile([P, K], U8, name="wq_s", align_bytes=64)
         nc.vector.tensor_copy(
             wq_s[:].rearrange("p (t c i) -> p c t i", t=PACK, i=16),
@@ -109,19 +108,23 @@ def tile_attend_tributaries_madefour_kernel(
         st = sb.tile([P, Q], U32, name="st", align_bytes=64)
         st_s = sb.tile([P, Q], U8, name="st_s", align_bytes=64)
         nc.vector.quantize_mx(st[:].bitcast(FP8X4), st_s[:], st_bf[:].rearrange("p q t -> p (q t)"))
+        f2 = shared.tile([P, T], F32, name="f2", align_bytes=64, offset=0)
+        nc.vector.memset(f2[:], 0.0)
 
-        qv_ps = ps.tile([P, PACK, Q], F32, name="qv_ps")
+        qv_ps = ps.tile([P, PACK, Q], F32, name="qv_ps", tag="bank_c0")
         for t in range(PACK):
             cols = slice(t * P, (t + 1) * P)
             nc.tensor.matmul_mx(
                 qv_ps[:, t, :], lhsT=wq[:, cols].bitcast(FP8X4), lhsT_scale=wq_s[:, cols],
                 rhs=st[:].bitcast(FP8X4), rhs_scale=st_s[:], start=True, stop=True,
             )
-        qv_bf = sb.tile([P, Q, PACK], BF16, name="qv_bf", align_bytes=64)
+        qv_bf = sb.tile([P, Q, PACK], BF16, name="qv_bf", tag="qv_bf", align_bytes=64)
         nc.vector.tensor_copy(qv_bf[:], qv_ps[:].rearrange("p t q -> p q t"))
         qv = sb.tile([P, Q], U32, name="qv", align_bytes=64)
         qv_s = sb.tile([P, Q], U8, name="qv_s", align_bytes=64)
         nc.vector.quantize_mx(qv[:].bitcast(FP8X4), qv_s[:], qv_bf[:].rearrange("p q t -> p (q t)"))
+        f3 = sb.tile([P, T], F32, name="f3", tag="qv_bf", align_bytes=64)
+        nc.vector.memset(f3[:], 0.0)
 
         def scores(tag, rows, rows_s, table, table_s, fp4, c0, c1):
             bank = ps.tile([P, c1 - c0], F32, name=tag + str(c0), tag=tag)
@@ -140,10 +143,12 @@ def tile_attend_tributaries_madefour_kernel(
         a = sb.tile([P, T], F32, name="a")
         a0 = scores("bank_x", qv, qv_s, keys, keys_s, True, 0, 512)
         a1 = scores("bank_y", qv, qv_s, keys, keys_s, True, 512, 768)
-        a2 = scores("bank_z", qv, qv_s, keys, keys_s, True, 768, 1024)
+        a2 = scores("bank_z", qv, qv_s, keys, keys_s, True, 768, 896)
+        a3 = scores("bank_w", qv, qv_s, keys, keys_s, True, 896, 1024)
         nc.vector.tensor_copy(a[:, 0:512], a0[:])
         nc.scalar.activation(a[:, 512:768], a1[:], COPY)
-        nc.scalar.activation(a[:, 768:1024], a2[:], COPY)
+        nc.scalar.activation(a[:, 768:896], a2[:], COPY)
+        nc.vector.tensor_copy(a[:, 896:1024], a3[:])
         ga = sb.tile([P, I], F32, name="ga")
         gather_halves(ga, a, l1)
         nc.vector.tensor_copy(f1[:].indirect(l3[:]), ga[:])

@@ -20,6 +20,9 @@ P = 128
 PACK = 4
 BANK = 512
 HALF = I // 2
+SIDE = 320
+MAIN = T - SIDE
+LEAD = 256
 
 
 def tile_attend_tributaries_madefour_kernel(
@@ -71,8 +74,8 @@ def tile_attend_tributaries_madefour_kernel(
 
         st_raw = sb.tile([P, PACK, Q], F32, name="st_raw")
         nc.sync.dma_start(st_raw[:], states.rearrange("(p j) q -> p j q", j=PACK))
-        load_scales(nc.sync, wq_raw_s, wq_scales)
         wq_raw = load_fp8("wq_raw", wq_words, K)
+        load_scales(nc.sync, wq_raw_s, wq_scales)
         load_scales(nc.sync, keys_s, keys_scales)
         keys = load_fp4("keys", keys_words)
         l1 = load_list("l1", offs)
@@ -119,10 +122,15 @@ def tile_attend_tributaries_madefour_kernel(
                 rhs=st[:].bitcast(FP8X4), rhs_scale=st_s[:], start=True, stop=True,
             )
         qv_bf = sb.tile([P, Q, PACK], BF16, name="qv_bf", tag="qv_bf", align_bytes=64)
-        nc.vector.tensor_copy(qv_bf[:], qv_ps[:].rearrange("p t q -> p q t"))
+        q_halves = [slice(0, Q // 2), slice(Q // 2, Q)]
+        for rows in q_halves:
+            nc.vector.tensor_copy(qv_bf[:, rows, :], qv_ps[:, :, rows].rearrange("p t q -> p q t"))
         qv = sb.tile([P, Q], U32, name="qv", align_bytes=64)
         qv_s = sb.tile([P, Q], U8, name="qv_s", align_bytes=64)
-        nc.vector.quantize_mx(qv[:].bitcast(FP8X4), qv_s[:], qv_bf[:].rearrange("p q t -> p (q t)"))
+        for rows in q_halves:
+            nc.vector.quantize_mx(
+                qv[:, rows].bitcast(FP8X4), qv_s[:, rows], qv_bf[:, rows, :].rearrange("p q t -> p (q t)")
+            )
         f3 = sb.tile([P, T], F32, name="f3", tag="qv_bf", align_bytes=64)
         nc.vector.memset(f3[:], 0.0)
 
@@ -153,7 +161,7 @@ def tile_attend_tributaries_madefour_kernel(
         gather_halves(ga, a, l1)
         nc.vector.tensor_copy(f1[:].indirect(l3[:]), ga[:])
 
-        b = sb.tile([P, T], F32, name="b")
+        b = sb.tile([P, T], F32, name="b", tag="b")
         for h in range(2):
             bank = scores("bank_b%d" % h, qv, qv_s, notes, notes_s, False, h * BANK, (h + 1) * BANK)
             nc.scalar.activation(b[:, h * BANK : (h + 1) * BANK], bank[:], COPY)
@@ -164,11 +172,15 @@ def tile_attend_tributaries_madefour_kernel(
         c_banks = [scores("bank_c%d" % h, st, st_s, users, users_s, True, h * BANK, (h + 1) * BANK) for h in range(2)]
         m1 = sb.tile([P, T], F32, name="m1")
         cc = sb.tile([P, T], F32, name="cc")
-        halves = [slice(h * BANK, (h + 1) * BANK) for h in range(2)]
-        for h in range(2):
-            nc.vector.tensor_tensor(m1[:, halves[h]], f1[:, halves[h]], f2[:, halves[h]], ALU.min)
-        for h in range(2):
-            nc.vector.tensor_tensor(cc[:, halves[h]], c_banks[h][:], m1[:, halves[h]], ALU.add)
+        side = slice(MAIN, T)
+        side_sums = sb.tile([P, 2, SIDE], F32, name="side_sums", tag="b")
+        nc.scalar.activation(side_sums[:, 0, :], c_banks[1][:, MAIN - BANK :], COPY)
+        for cols in (slice(0, LEAD), side, slice(LEAD, MAIN)):
+            nc.vector.tensor_tensor(m1[:, cols], f1[:, cols], f2[:, cols], ALU.min)
+        nc.gpsimd.tensor_tensor(cc[:, side], side_sums[:, 0, :], m1[:, side], ALU.add)
+        nc.vector.tensor_tensor(cc[:, :LEAD], c_banks[0][:, :LEAD], m1[:, :LEAD], ALU.add)
+        nc.vector.tensor_tensor(cc[:, LEAD:BANK], c_banks[0][:, LEAD:], m1[:, LEAD:BANK], ALU.add)
+        nc.vector.tensor_tensor(cc[:, BANK:MAIN], c_banks[1][:, : MAIN - BANK], m1[:, BANK:MAIN], ALU.add)
         gc = sb.tile([P, I], F32, name="gc")
         gather_halves(gc, cc, l5)
         nc.vector.tensor_copy(f3[:].indirect(l6[:]), gc[:])
@@ -178,8 +190,10 @@ def tile_attend_tributaries_madefour_kernel(
             for h, tag in enumerate(("bank_x", "bank_y"))
         ]
         dd = sb.tile([P, T], F32, name="dd")
-        for h in range(2):
-            nc.vector.tensor_tensor(dd[:, halves[h]], d_banks[h][:], f3[:, halves[h]], ALU.subtract)
+        nc.scalar.activation(side_sums[:, 1, :], d_banks[1][:, MAIN - BANK :], COPY)
+        nc.gpsimd.tensor_tensor(dd[:, side], side_sums[:, 1, :], f3[:, side], ALU.subtract)
+        nc.vector.tensor_tensor(dd[:, :BANK], d_banks[0][:], f3[:, :BANK], ALU.subtract)
+        nc.vector.tensor_tensor(dd[:, BANK:MAIN], d_banks[1][:, : MAIN - BANK], f3[:, BANK:MAIN], ALU.subtract)
         y = sb.tile([P, I], F32, name="y")
         gather_halves(y, dd, l7)
         nc.sync.dma_start(out[:, :HALF], y[:, :HALF])

from contextlib import ExitStack

import concourse.mybir as mybir

D, K, T, I, Q = 512, 512, 1024, 512, 128
FLOPS = 2 * D * K * Q + 4 * 2 * K * Q * T

F32 = mybir.dt.float32
BF16 = mybir.dt.bfloat16
I32 = mybir.dt.int32
U32 = mybir.dt.uint32
U16 = mybir.dt.uint16
U8 = mybir.dt.uint8
FP8X4 = mybir.dt.float8_e4m3fn_x4
FP4X4 = mybir.dt.float4_e2m1fn_x4
COPY = mybir.ActivationFunctionType.Copy
ALU = mybir.AluOpType

P = 128
PACK = 4
BANK = 512
HALF = I // 2
SIDE = 320
MAIN = T - SIDE
LEAD = 256


def tile_attend_tributaries_madefour_kernel(
    tc, states, wq_words, wq_scales, keys_words, keys_scales, notes_words, notes_scales,
    users_words, users_scales, shelves_words, shelves_scales,
    offs, offs2, offs3, offs4, offs5, offs6, offs7, out,
):
    nc = tc.nc
    with ExitStack() as ctx:
        sb = ctx.enter_context(tc.tile_pool(name="sb", bufs=1))
        shared = ctx.enter_context(tc.tile_pool(name="shared", bufs=1))
        ps = ctx.enter_context(tc.psum_pool(name="ps", bufs=1))

        def zeroed_plane(engine, name, width):
            plane = sb.tile([P, width], U8, name=name, align_bytes=64)
            engine.memset(plane[:].bitcast(I32), 0)
            return plane

        def load_scales(queue, plane, scales):
            for quad in range(4):
                queue.dma_start(
                    plane[32 * quad : 32 * quad + 4, :].bitcast(I32),
                    scales[0, 4 * quad : 4 * quad + 4, :].bitcast(I32),
                )

        def load_fp8(name, words, width):
            codes = sb.tile([P, width], U32, name=name, align_bytes=64)
            nc.sync.dma_start(codes[:].bitcast(I32), words[0].rearrange("p n t -> p (n t)").bitcast(I32))
            return codes

        def load_fp4(name, words):
            codes = sb.tile([P, 2 * T], U8, name=name, align_bytes=64)
            nc.sync.dma_start(codes[:].bitcast(I32), words[0].bitcast(I32))
            return codes

        def load_list(name, src):
            lst = sb.tile([P, I // 16], U16, name=name)
            nc.sync.dma_start(lst[:], src)
            return lst

        wq_raw_s = shared.tile([P, K], U8, name="wq_raw_s", align_bytes=64, offset=0)
        nc.gpsimd.memset(wq_raw_s[:].bitcast(I32), 0)
        keys_s = zeroed_plane(nc.gpsimd, "keys_s", T)
        notes_s = zeroed_plane(nc.vector, "notes_s", T)
        users_s = zeroed_plane(nc.vector, "users_s", T)
        shelves_s = zeroed_plane(nc.vector, "shelves_s", T)
        f1 = sb.tile([P, T], F32, name="f1")
        nc.vector.memset(f1[:], 0.0)

        st_raw = sb.tile([P, PACK, Q], F32, name="st_raw")
        nc.sync.dma_start(st_raw[:], states.rearrange("(p j) q -> p j q", j=PACK))
        wq_raw = load_fp8("wq_raw", wq_words, K)
        load_scales(nc.sync, wq_raw_s, wq_scales)
        load_scales(nc.sync, keys_s, keys_scales)
        keys = load_fp4("keys", keys_words)
        l1 = load_list("l1", offs)
        l3 = load_list("l3", offs3)
        notes = load_fp8("notes", notes_words, T)
        load_scales(nc.sync, notes_s, notes_scales)
        l2 = load_list("l2", offs2)
        l4 = load_list("l4", offs4)
        users = load_fp4("users", users_words)
        load_scales(nc.sync, users_s, users_scales)
        l5 = load_list("l5", offs5)
        l6 = load_list("l6", offs6)
        shelves = load_fp8("shelves", shelves_words, T)
        load_scales(nc.sync, shelves_s, shelves_scales)
        l7 = load_list("l7", offs7)

        st_bf = shared.tile([P, Q, PACK], BF16, name="st_bf", align_bytes=64, offset=K)
        nc.vector.tensor_copy(
            st_bf[:].rearrange("p (c i) t -> p c t i", i=4),
            st_raw[:].rearrange("p t (c i) -> p c t i", i=4),
        )
        wq = sb.tile([P, K], U32, name="wq", align_bytes=64)
        for pair in range(2):
            nc.scalar.copy(
                wq[:, 256 * pair : 256 * (pair + 1)].rearrange("p (t c i) -> p c t i", t=2, i=4),
                wq_raw[:].rearrange("p (c i t) -> p c t i", t=PACK, i=4)[:, :, 2 * pair : 2 * pair + 2, :],
            )
        wq_s = sb.tile([P, K], U8, name="wq_s", align_bytes=64)
        nc.vector.tensor_copy(
            wq_s[:].rearrange("p (t c i) -> p c t i", t=PACK, i=16),
            wq_raw_s[:].rearrange("p (c i t) -> p c t i", t=PACK, i=16),
        )
        st = sb.tile([P, Q], U32, name="st", align_bytes=64)
        st_s = sb.tile([P, Q], U8, name="st_s", align_bytes=64)
        nc.vector.quantize_mx(st[:].bitcast(FP8X4), st_s[:], st_bf[:].rearrange("p q t -> p (q t)"))
        f2 = shared.tile([P, T], F32, name="f2", align_bytes=64, offset=0)
        nc.vector.memset(f2[:], 0.0)

        qv_ps = ps.tile([P, PACK, Q], F32, name="qv_ps", tag="bank_c0")
        for t in range(PACK):
            cols = slice(t * P, (t + 1) * P)
            nc.tensor.matmul_mx(
                qv_ps[:, t, :], lhsT=wq[:, cols].bitcast(FP8X4), lhsT_scale=wq_s[:, cols],
                rhs=st[:].bitcast(FP8X4), rhs_scale=st_s[:], start=True, stop=True,
            )
        qv_bf = sb.tile([P, Q, PACK], BF16, name="qv_bf", tag="qv_bf", align_bytes=64)
        q_halves = [slice(0, Q // 2), slice(Q // 2, Q)]
        for rows in q_halves:
            nc.vector.tensor_copy(qv_bf[:, rows, :], qv_ps[:, :, rows].rearrange("p t q -> p q t"))
        qv = sb.tile([P, Q], U32, name="qv", align_bytes=64)
        qv_s = sb.tile([P, Q], U8, name="qv_s", align_bytes=64)
        for rows in q_halves:
            nc.vector.quantize_mx(
                qv[:, rows].bitcast(FP8X4), qv_s[:, rows], qv_bf[:, rows, :].rearrange("p q t -> p (q t)")
            )
        f3 = sb.tile([P, T], F32, name="f3", tag="qv_bf", align_bytes=64)
        nc.vector.memset(f3[:], 0.0)

        def scores(tag, rows, rows_s, table, table_s, fp4, c0, c1):
            bank = ps.tile([P, c1 - c0], F32, name=tag + str(c0), tag=tag)
            moving = table[:, 2 * c0 : 2 * c1].bitcast(FP4X4) if fp4 else table[:, c0:c1].bitcast(FP8X4)
            nc.tensor.matmul_mx(
                bank[:], lhsT=rows[:].bitcast(FP8X4), lhsT_scale=rows_s[:],
                rhs=moving, rhs_scale=table_s[:, c0:c1], start=True, stop=True,
            )
            return bank

        def gather_halves(dst, window, lst):
            cols = HALF // 16
            nc.vector.tensor_copy(dst[:, :HALF], window[:].indirect(lst[:, :cols]))
            nc.scalar.activation(dst[:, HALF:], window[:].indirect(lst[:, cols:]), COPY)

        a = sb.tile([P, T], F32, name="a")
        a0 = scores("bank_x", qv, qv_s, keys, keys_s, True, 0, 512)
        a1 = scores("bank_y", qv, qv_s, keys, keys_s, True, 512, 768)
        a2 = scores("bank_z", qv, qv_s, keys, keys_s, True, 768, 896)
        a3 = scores("bank_w", qv, qv_s, keys, keys_s, True, 896, 1024)
        nc.vector.tensor_copy(a[:, 0:512], a0[:])
        nc.scalar.activation(a[:, 512:768], a1[:], COPY)
        nc.scalar.activation(a[:, 768:896], a2[:], COPY)
        nc.vector.tensor_copy(a[:, 896:1024], a3[:])
        ga = sb.tile([P, I], F32, name="ga")
        gather_halves(ga, a, l1)
        nc.vector.tensor_copy(f1[:].indirect(l3[:]), ga[:])

        b = sb.tile([P, T], F32, name="b", tag="b")
        for h in range(2):
            bank = scores("bank_b%d" % h, qv, qv_s, notes, notes_s, False, h * BANK, (h + 1) * BANK)
            nc.scalar.activation(b[:, h * BANK : (h + 1) * BANK], bank[:], COPY)
        gb = sb.tile([P, I], F32, name="gb")
        nc.scalar.activation(gb[:], b[:].indirect(l2[:]), COPY)
        nc.vector.tensor_copy(f2[:].indirect(l4[:]), gb[:])

        c_banks = [scores("bank_c%d" % h, st, st_s, users, users_s, True, h * BANK, (h + 1) * BANK) for h in range(2)]
        m1 = sb.tile([P, T], F32, name="m1")
        cc = sb.tile([P, T], F32, name="cc")
        side = slice(MAIN, T)
        side_sums = sb.tile([P, 2, SIDE], F32, name="side_sums", tag="b")
        nc.scalar.activation(side_sums[:, 0, :], c_banks[1][:, MAIN - BANK :], COPY)
        for cols in (slice(0, LEAD), side, slice(LEAD, MAIN)):
            nc.vector.tensor_tensor(m1[:, cols], f1[:, cols], f2[:, cols], ALU.min)
        nc.gpsimd.tensor_tensor(cc[:, side], side_sums[:, 0, :], m1[:, side], ALU.add)
        nc.vector.tensor_tensor(cc[:, :LEAD], c_banks[0][:, :LEAD], m1[:, :LEAD], ALU.add)
        nc.vector.tensor_tensor(cc[:, LEAD:BANK], c_banks[0][:, LEAD:], m1[:, LEAD:BANK], ALU.add)
        nc.vector.tensor_tensor(cc[:, BANK:MAIN], c_banks[1][:, : MAIN - BANK], m1[:, BANK:MAIN], ALU.add)
        gc = sb.tile([P, I], F32, name="gc")
        gather_halves(gc, cc, l5)
        nc.vector.tensor_copy(f3[:].indirect(l6[:]), gc[:])

        d_banks = [
            scores(tag, st, st_s, shelves, shelves_s, False, h * BANK, (h + 1) * BANK)
            for h, tag in enumerate(("bank_x", "bank_y"))
        ]
        dd = sb.tile([P, T], F32, name="dd")
        nc.scalar.activation(side_sums[:, 1, :], d_banks[1][:, MAIN - BANK :], COPY)
        nc.gpsimd.tensor_tensor(dd[:, side], side_sums[:, 1, :], f3[:, side], ALU.subtract)
        nc.vector.tensor_tensor(dd[:, :BANK], d_banks[0][:], f3[:, :BANK], ALU.subtract)
        nc.vector.tensor_tensor(dd[:, BANK:MAIN], d_banks[1][:, : MAIN - BANK], f3[:, BANK:MAIN], ALU.subtract)
        y = sb.tile([P, I], F32, name="y")
        gather_halves(y, dd, l7)
        nc.sync.dma_start(out[:, :HALF], y[:, :HALF])
        nc.scalar.dma_start(out[:, HALF:], y[:, HALF:])
